import numpy as np
import ml_dtypes


def mxq(x, axis, fmt="e4m3"):
    dtype, down = {"e4m3": (ml_dtypes.float8_e4m3fn, 7), "e5m2": (ml_dtypes.float8_e5m2, 14)}[fmt]
    v = np.moveaxis(np.asarray(x, np.float32).astype(ml_dtypes.bfloat16).astype(np.float64), axis, -1)
    blocks = v.reshape(v.shape[:-1] + (-1, 32))
    amax = np.abs(blocks).max(-1, keepdims=True)
    byte = np.maximum(np.where(amax > 0, np.frexp(amax)[1] - 1 + 127, 0) - down, 1)
    scale = np.exp2(byte - 127.0)
    codes = (blocks / scale).astype(np.float32).astype(dtype).astype(np.float64)
    return np.moveaxis((codes * scale).reshape(v.shape), -1, axis)


WIDE = False


def mx_kscale(k):
    if not WIDE:
        return np.ones(k)
    levels = np.array([10, -10, 5, -5, 0])
    if k % 512:
        return np.exp2(np.random.permutation(np.resize(levels, k // 32))).repeat(32)
    a = np.empty((k // 512, 16))
    for p in range(k // 512):
        a[p, :8] = np.random.permutation(np.resize(levels, 8))
        for g in range(8):
            far = levels[np.abs(levels - a[p, g]) >= 10]
            a[p, g + 8] = far[np.random.randint(len(far))]
    return np.exp2(a.ravel()).repeat(32)


def f64(x):
    return np.asarray(x).astype(np.float64)


def striped(idx):
    return np.tile(idx.reshape(-1, 16).T, (8, 1)).astype(np.uint16)


def unstriped(offs):
    return offs[:16].T.reshape(-1).astype(np.int64)


def striped8(idx):
    return np.concatenate([x.reshape(-1, 16).T for x in idx]).astype(np.uint16)


def runs(offs, k):
    lists = np.stack([offs[16 * r : 16 * r + 16].T.reshape(-1) for r in range(8)]).astype(np.int64)
    return lists[np.arange(k) % 512 // 64]


def pack_weight(w):
    k, n = w.shape
    w = f64(np.asarray(w, np.float32).astype(ml_dtypes.bfloat16)).reshape(k // 32, 32, n)
    amax = np.abs(w).max(1)
    byte = np.clip(np.where(amax > 0, np.frexp(amax)[1] - 1 + 127 - 7, 1), 1, 254)
    scaled = (w * np.exp2(127.0 - byte)[:, None, :]).reshape(k, n).astype(np.float32)
    words = np.ascontiguousarray(scaled.reshape(k // 512, 128, 4, n).transpose(0, 1, 3, 2)).astype(ml_dtypes.float8_e4m3fn).view(np.uint8)
    return words, np.ascontiguousarray(byte.astype(np.uint8).reshape(k // 512, 16, n))


def unpack_weight(words, scales):
    g, p, n, _ = words.shape
    vals = np.ascontiguousarray(words).view(ml_dtypes.float8_e4m3fn).astype(np.float64) * np.repeat(np.exp2(scales.astype(np.float64) - 127.0), 8, axis=1)[..., None]
    return vals.transpose(0, 1, 3, 2).reshape(g * 512, n)


def relu(v):
    return np.maximum(v, 0.0)


K, T, S, N, H = 512, 2048, 512, 512, 512


def setup_inputs():
    n = np.random.standard_normal
    s = mx_kscale(K)[:, None]
    u = mx_kscale(H)
    packed_xT = pack_weight(n((K, T)) * s)
    return {
        "x_words": packed_xT[0],
        "x_scales": packed_xT[1],
        "w1": (n((K, H)) / np.sqrt(K) / s * u).astype(np.float32),
        "eps": np.random.uniform(1.0, 1.5, (H, 1)).astype(np.float32),
        "w2": (n((H, H)) / np.sqrt(H) / u[:, None] * u).astype(np.float32),
        "res": (2 * n((N, S))).astype(np.float32),
        "w3": (n((H, N)) / np.sqrt(H) / u[:, None]).astype(np.float32),
        "offs": striped(np.random.permutation(T)[:S]),
        "p1": striped8(np.stack([np.random.permutation(S) for _ in range(8)])),
        "p2": striped8(np.stack([np.random.permutation(S) for _ in range(8)])),
    }


def reference(x_words, x_scales, w1, eps, w2, res, w3, offs, p1, p2):
    xq = unpack_weight(x_words, x_scales)[:, unstriped(offs)]
    y = mxq(f64(w1), 0, "e4m3").T @ xq
    z = f64(eps) * y + y[np.arange(H)[:, None], runs(p1, H)] + y[np.arange(H)[:, None], runs(p2, H)]
    h = relu(mxq(f64(w2), 0, "e4m3").T @ mxq(z, 0, "e4m3"))
    return f64(res) + (mxq(f64(w3), 0, "e4m3").T @ mxq(h, 0, "e4m3"))

@@ -1,0 +1,218 @@
+from contextlib import ExitStack
+
+import concourse.mybir as mybir
+from concourse.masks import make_identity
+
+K, T, S, H, N = 512, 2048, 512, 512, 512
+FLOPS = 2 * S * (K * H + H * H + H * N)
+
+F32 = mybir.dt.float32
+BF16 = mybir.dt.bfloat16
+I32 = mybir.dt.int32
+U32 = mybir.dt.uint32
+U16 = mybir.dt.uint16
+U8 = mybir.dt.uint8
+FP8X4 = mybir.dt.float8_e4m3fn_x4
+COPY = mybir.ActivationFunctionType.Copy
+RELU = mybir.ActivationFunctionType.Relu
+ADD = mybir.AluOpType.add
+MULT = mybir.AluOpType.mult
+
+P = 128
+PACK = 4
+HALF = S // 2
+BLOCK = 128
+BLOCKS = S // BLOCK
+PIECES = ((0, 256), (256, 384), (384, 512))
+SUM_BANK = (0, 1, 0, 5)
+BACK_BANK = (4, 5, 4, 6)
+HIDDEN_BANK = (7, 2, 3, 1)
+OUT_BANK = (0, 4, 5, 6)
+
+
+def tile_picked_gin8_relu_p_kernel(
+    tc, x_words, x_scales, w1, eps, w2, res, w3, offs, p1, p2, out
+):
+    nc = tc.nc
+    with ExitStack() as ctx:
+        lists = ctx.enter_context(tc.tile_pool(name="lists", bufs=1))
+        keep = ctx.enter_context(tc.tile_pool(name="keep", bufs=1))
+        psum = ctx.enter_context(tc.psum_pool(name="psum", bufs=1))
+
+        def bank(b, shape, name):
+            return psum.tile(shape, F32, name=name, tag=f"bank{b}")
+
+        def tile(shape, dtype, name, tag=None):
+            return keep.tile(shape, dtype, name=name, tag=tag or name, align_bytes=64)
+
+        offs_t = lists.tile([P, S // 16], U16, name="offs_t")
+        p1_t = lists.tile([P, S // 16], U16, name="p1_t")
+        p2_t = lists.tile([P, S // 16], U16, name="p2_t")
+
+        x_table = tile([P, T], U32, "x_table", "slot_c")
+        scale_table = tile([P, T], U8, "scale_table", "slot_a")
+        w1_raw = tile([P, PACK, H], F32, "w1_raw", "slot_b")
+        eps_t = tile([P, PACK], F32, "eps_t")
+        ident = tile([P, P], F32, "ident")
+        warm = tile([P, 1], F32, "warm")
+
+        nc.gpsimd.memset(scale_table[:].bitcast(I32), 0)
+        make_identity(nc, ident[:])
+        nc.scalar.activation(warm[:], ident[:, 0:1], RELU)
+
+        nc.sync.dma_start(offs_t[:], offs)
+        nc.sync.dma_start(w1_raw[:], w1.rearrange("(p j) c -> p j c", j=PACK))
+        for q in range(4):
+            nc.sync.dma_start(
+                scale_table[32 * q : 32 * q + 4, :].bitcast(I32),
+                x_scales[0, 4 * q : 4 * q + 4, :].bitcast(I32),
+            )
+        nc.sync.dma_start(
+            x_table[:].bitcast(I32), x_words[0].rearrange("p n t -> p (n t)").bitcast(I32)
+        )
+        nc.gpsimd.dma_start(eps_t[:], eps.rearrange("(p t) o -> p (t o)", t=PACK))
+        nc.sync.dma_start(p1_t[:], p1)
+        nc.sync.dma_start(p2_t[:], p2)
+
+        def deal_columns(copy, raw, u, name):
+            grouped = tile([P, 2, P, PACK], BF16, name)
+            copy(
+                grouped[:].rearrange("p e m j -> p m j e"),
+                raw[:].rearrange("p j (m t) -> p m j t", t=PACK)[:, :, :, 2 * u : 2 * u + 2],
+            )
+            return grouped[:].rearrange("p e m j -> p (e m j)")
+
+        def quantize(codes, scales, values):
+            nc.vector.quantize_mx(out=codes.bitcast(FP8X4), scales=scales, in_=values)
+
+        def product(acc, weights, t, codes, scales):
+            cols = slice(P * t, P * (t + 1))
+            nc.tensor.matmul_mx(
+                out=acc,
+                lhsT=weights[0][:, cols].bitcast(FP8X4),
+                lhsT_scale=weights[1][:, cols],
+                rhs=codes.bitcast(FP8X4),
+                rhs_scale=scales,
+                start=True,
+                stop=True,
+            )
+
+        def quantize_halves(halves, name, tag=None):
+            codes = tile([P, H], U32, name + "_codes", tag)
+            scales = tile([P, H], U8, name + "_scales")
+            for u in range(2):
+                cols = slice(2 * P * u, 2 * P * (u + 1))
+                quantize(codes[:, cols], scales[:, cols], halves[u])
+            return codes, scales
+
+        x_scale = tile([P, S], U8, "x_scale")
+        nc.vector.tensor_copy(x_scale[:], scale_table[:].indirect(offs_t[:]))
+        w1_mx = quantize_halves(
+            [deal_columns(copy, w1_raw, u, f"w1_grouped{u}") for u, copy in enumerate((nc.vector.tensor_copy, nc.scalar.copy))],
+            "w1",
+        )
+
+        x_codes = []
+        for h in range(2):
+            codes = tile([P, HALF], U32, f"x_codes{h}")
+            nc.vector.tensor_copy(
+                codes[:], x_table[:].indirect(offs_t[:, h * HALF // 16 : (h + 1) * HALF // 16])
+            )
+            x_codes.append(codes)
+
+        w2_raw = tile([P, PACK, H], F32, "w2_raw", "slot_a")
+        nc.sync.dma_start(w2_raw[:], w2.rearrange("(p j) c -> p j c", j=PACK))
+        w3_raw = tile([P, PACK, N], F32, "w3_raw", "slot_b")
+        nc.sync.dma_start(w3_raw[:], w3.rearrange("(p j) c -> p j c", j=PACK))
+        res_t = tile([P, PACK, S], F32, "res_t", "slot_c")
+        nc.sync.dma_start(res_t[:], res.rearrange("(t p) s -> p t s", t=PACK))
+
+        y = [tile([P, S], F32, f"y{t}") for t in range(PACK)]
+        own = [tile([P, S], F32, f"own{t}") for t in range(PACK)]
+        for pair in range(2):
+            for h in range(2):
+                for t in (2 * pair, 2 * pair + 1):
+                    acc = bank(4 * h + t, [P, HALF], f"y_acc{h}{t}")
+                    cols = slice(h * HALF, (h + 1) * HALF)
+                    product(acc[:], w1_mx, t, x_codes[h][:], x_scale[:, cols])
+                    if h == 1 and t == 0:
+                        nc.vector.tensor_copy(y[t][:, cols], acc[:])
+                    else:
+                        nc.scalar.copy(y[t][:, cols], acc[:])
+        for t in range(PACK):
+            nc.scalar.activation(own[t][:], y[t][:], COPY, scale=eps_t[:, t : t + 1])
+
+        w3_grouped = tile([P, N, PACK], BF16, "w3_grouped")
+        for t in range(PACK):
+            cols = slice(P * t, P * (t + 1))
+            nc.gpsimd.tensor_scalar(
+                w3_grouped[:, cols, :], w3_raw[:, :, cols].rearrange("p j c -> p c j"), 1.0, 0.0, MULT, ADD
+            )
+
+        def turn_into(acc, source, start, stop):
+            nc.tensor.matmul(acc, lhsT=source, rhs=ident[:], is_transpose=True, start=start, stop=stop)
+
+        def turn_back(b, z_turned):
+            z_rows = tile([P, 2, P, 2], BF16, f"z_rows{b}")
+            nc.scalar.copy(z_rows[:], z_turned[:].rearrange("s (u e) p -> s u p e", e=2))
+            words = z_rows[:].rearrange("s u p e -> s (u p e)").bitcast(F32)
+            back = bank(BACK_BANK[b], [P, 2, BLOCK], f"back{b}")
+            for u in range(2):
+                nc.tensor.transpose(back[:, u, :], words[:, u * P : (u + 1) * P], ident[:])
+            z_grouped = tile([P, BLOCK * PACK], BF16, f"z_grouped{b}")
+            nc.scalar.copy(
+                z_grouped[:].bitcast(F32).rearrange("p (s u) -> p s u", u=2),
+                back[:].rearrange("p u s -> p s u"),
+            )
+            return z_grouped
+
+        z_grouped = []
+        for lo, hi in PIECES:
+            z_turned = {}
+            for b in range(lo // BLOCK, hi // BLOCK):
+                z_turned[b] = bank(SUM_BANK[b], [P, PACK, P], f"z_turned{b}")
+                for t in range(PACK):
+                    turn_into(z_turned[b][:, t, :], own[t][:, b * BLOCK : (b + 1) * BLOCK], t == 0, False)
+            for t in range(PACK):
+                for name, places in (("a", p1_t), ("b", p2_t)):
+                    fetched = tile([P, hi - lo], F32, f"fetched_{name}{t}_{lo}")
+                    nc.vector.tensor_copy(fetched[:], y[t][:].indirect(places[:, lo // 16 : hi // 16]))
+                    for c in range(lo, hi, BLOCK):
+                        turn_into(
+                            z_turned[c // BLOCK][:, t, :],
+                            fetched[:, c - lo : c - lo + BLOCK],
+                            False,
+                            t == PACK - 1 and name == "b",
+                        )
+            for b in range(lo // BLOCK, hi // BLOCK):
+                z_grouped.append(turn_back(b, z_turned[b]))
+
+        w2_halves = [deal_columns(nc.scalar.copy, w2_raw, u, f"w2_grouped{u}") for u in range(2)]
+        w2_mx = quantize_halves(w2_halves, "w2", "fetched_b3_384")
+        w3_mx = (tile([P, N], U32, "w3_codes", "z_rows3"), tile([P, N], U8, "w3_scales"))
+        quantize(w3_mx[0][:], w3_mx[1][:], w3_grouped[:].rearrange("p c j -> p (c j)"))
+
+        out_rows = out.rearrange("(t p) s -> p t s", t=PACK)
+        for b in range(BLOCKS):
+            cols = slice(b * BLOCK, (b + 1) * BLOCK)
+            z_codes = tile([P, BLOCK], U32, f"z_codes{b}")
+            z_scales = tile([P, BLOCK], U8, f"z_scales{b}")
+            quantize(z_codes[:], z_scales[:], z_grouped[b][:])
+            h_acc = bank(HIDDEN_BANK[b], [P, PACK, BLOCK], f"h_acc{b}")
+            for t in range(PACK):
+                product(h_acc[:, t, :], w2_mx, t, z_codes[:], z_scales[:])
+            h_grouped = tile([P, BLOCK * PACK], BF16, f"h_grouped{b}")
+            nc.scalar.activation(
+                h_grouped[:].rearrange("p (s t) -> p s t", t=PACK),
+                h_acc[:].rearrange("p t s -> p s t"),
+                RELU,
+            )
+            h_codes = tile([P, BLOCK], U32, f"h_codes{b}")
+            h_scales = tile([P, BLOCK], U8, f"h_scales{b}")
+            quantize(h_codes[:], h_scales[:], h_grouped[:])
+            o_acc = bank(OUT_BANK[b], [P, PACK, BLOCK], f"o_acc{b}")
+            for t in range(PACK):
+                product(o_acc[:, t, :], w3_mx, t, h_codes[:], h_scales[:])
+            result = tile([P, PACK, BLOCK], F32, f"result{b}")
+            nc.vector.tensor_tensor(result[:], o_acc[:], res_t[:, :, cols], ADD)
+            nc.sync.dma_start(out_rows[:, :, cols], result[:])

@@ -1,7 +1,6 @@
 from contextlib import ExitStack
 
 import concourse.mybir as mybir
-from concourse.masks import make_identity
 
 K, T, S, H, N = 512, 2048, 512, 512, 512
 FLOPS = 2 * S * (K * H + H * H + H * N)
@@ -16,18 +15,12 @@ FP8X4 = mybir.dt.float8_e4m3fn_x4
 COPY = mybir.ActivationFunctionType.Copy
 RELU = mybir.ActivationFunctionType.Relu
 ADD = mybir.AluOpType.add
-MULT = mybir.AluOpType.mult
 
 P = 128
 PACK = 4
 HALF = S // 2
 BLOCK = 128
 BLOCKS = S // BLOCK
-PIECES = ((0, 256), (256, 384), (384, 512))
-SUM_BANK = (0, 1, 0, 5)
-BACK_BANK = (4, 5, 4, 6)
-HIDDEN_BANK = (7, 2, 3, 1)
-OUT_BANK = (0, 4, 5, 6)
 
 
 def tile_picked_gin8_relu_p_kernel(
@@ -53,12 +46,8 @@ def tile_picked_gin8_relu_p_kernel(
         scale_table = tile([P, T], U8, "scale_table", "slot_a")
         w1_raw = tile([P, PACK, H], F32, "w1_raw", "slot_b")
         eps_t = tile([P, PACK], F32, "eps_t")
-        ident = tile([P, P], F32, "ident")
-        warm = tile([P, 1], F32, "warm")
 
         nc.gpsimd.memset(scale_table[:].bitcast(I32), 0)
-        make_identity(nc, ident[:])
-        nc.scalar.activation(warm[:], ident[:, 0:1], RELU)
 
         nc.sync.dma_start(offs_t[:], offs)
         nc.sync.dma_start(w1_raw[:], w1.rearrange("(p j) c -> p j c", j=PACK))
@@ -70,149 +59,170 @@ def tile_picked_gin8_relu_p_kernel(
         nc.sync.dma_start(
             x_table[:].bitcast(I32), x_words[0].rearrange("p n t -> p (n t)").bitcast(I32)
         )
-        nc.gpsimd.dma_start(eps_t[:], eps.rearrange("(p t) o -> p (t o)", t=PACK))
         nc.sync.dma_start(p1_t[:], p1)
         nc.sync.dma_start(p2_t[:], p2)
-
-        def deal_columns(copy, raw, u, name):
-            grouped = tile([P, 2, P, PACK], BF16, name)
-            copy(
-                grouped[:].rearrange("p e m j -> p m j e"),
-                raw[:].rearrange("p j (m t) -> p m j t", t=PACK)[:, :, :, 2 * u : 2 * u + 2],
-            )
-            return grouped[:].rearrange("p e m j -> p (e m j)")
-
-        def quantize(codes, scales, values):
-            nc.vector.quantize_mx(out=codes.bitcast(FP8X4), scales=scales, in_=values)
+        nc.gpsimd.dma_start(eps_t[:], eps.rearrange("(p t) o -> p (t o)", t=PACK))
 
         def product(acc, weights, t, codes, scales):
-            cols = slice(P * t, P * (t + 1))
+            lhs_codes, lhs_scales = weights[t]
             nc.tensor.matmul_mx(
                 out=acc,
-                lhsT=weights[0][:, cols].bitcast(FP8X4),
-                lhsT_scale=weights[1][:, cols],
+                lhsT=lhs_codes.bitcast(FP8X4),
+                lhsT_scale=lhs_scales,
                 rhs=codes.bitcast(FP8X4),
                 rhs_scale=scales,
                 start=True,
                 stop=True,
             )
 
-        def quantize_halves(halves, name, tag=None):
-            codes = tile([P, H], U32, name + "_codes", tag)
-            scales = tile([P, H], U8, name + "_scales")
-            for u in range(2):
-                cols = slice(2 * P * u, 2 * P * (u + 1))
-                quantize(codes[:, cols], scales[:, cols], halves[u])
+        def quantized(values, name, tag=None):
+            width = values.shape[1] // PACK
+            codes = tile([P, width], U32, name + "_codes", tag)
+            scales = tile([P, width], U8, name + "_scales")
+            nc.vector.quantize_mx(out=codes[:].bitcast(FP8X4), scales=scales[:], in_=values)
             return codes, scales
+
+        def column_tiles(codes, scales):
+            return [(codes[:, c : c + P], scales[:, c : c + P]) for c in range(0, codes.shape[1], P)]
+
+        def deal_columns(raw, grouped, u):
+            nc.scalar.activation(
+                grouped.rearrange("p e m j -> p m j e"),
+                raw[:].rearrange("p j (m t) -> p m j t", t=PACK)[:, :, :, 2 * u : 2 * u + 2],
+                COPY,
+            )
+
+        def deal_all_columns(raw, name):
+            grouped = tile([P, PACK, P, PACK], BF16, name)
+            nc.scalar.activation(
+                grouped[:].rearrange("p t m j -> p m j t"),
+                raw[:].rearrange("p j (m t) -> p m j t", t=PACK),
+                COPY,
+            )
+            return grouped[:].rearrange("p t m j -> p (t m j)")
 
         x_scale = tile([P, S], U8, "x_scale")
         nc.vector.tensor_copy(x_scale[:], scale_table[:].indirect(offs_t[:]))
-        w1_mx = quantize_halves(
-            [deal_columns(copy, w1_raw, u, f"w1_grouped{u}") for u, copy in enumerate((nc.vector.tensor_copy, nc.scalar.copy))],
-            "w1",
-        )
+        w1_grouped = [tile([P, 2, P, PACK], BF16, f"w1_grouped{u}") for u in range(2)]
+        for u in range(2):
+            deal_columns(w1_raw, w1_grouped[u][:], u)
+        w1_mx = column_tiles(*quantized(w1_grouped[0][:].rearrange("p e m j -> p (e m j)"), "w1_low"))
 
         x_codes = []
         for h in range(2):
-            codes = tile([P, HALF], U32, f"x_codes{h}")
+            codes = tile([P, HALF], U32, f"x_codes{h}", ("x_codes0", "w2_grouped")[h])
             nc.vector.tensor_copy(
                 codes[:], x_table[:].indirect(offs_t[:, h * HALF // 16 : (h + 1) * HALF // 16])
             )
             x_codes.append(codes)
 
+        w1_mx = w1_mx + column_tiles(
+            *quantized(w1_grouped[1][:].rearrange("p e m j -> p (e m j)"), "w1_high", "slot_c")
+        )
+
         w2_raw = tile([P, PACK, H], F32, "w2_raw", "slot_a")
         nc.sync.dma_start(w2_raw[:], w2.rearrange("(p j) c -> p j c", j=PACK))
         w3_raw = tile([P, PACK, N], F32, "w3_raw", "slot_b")
         nc.sync.dma_start(w3_raw[:], w3.rearrange("(p j) c -> p j c", j=PACK))
-        res_t = tile([P, PACK, S], F32, "res_t", "slot_c")
-        nc.sync.dma_start(res_t[:], res.rearrange("(t p) s -> p t s", t=PACK))
 
         y = [tile([P, S], F32, f"y{t}") for t in range(PACK)]
-        own = [tile([P, S], F32, f"own{t}") for t in range(PACK)]
-        for pair in range(2):
+        own = [[tile([P, HALF], F32, f"own{h}{t}") for t in range(PACK)] for h in range(2)]
+
+        def scale_own(h, t, acc):
+            nc.scalar.activation(own[h][t][:], acc, COPY, scale=eps_t[:, t : t + 1])
+
+        second_half = []
+        for h in range(2):
+            for t in range(2):
+                acc = bank(2 * h + t, [P, HALF], f"y_acc{h}{t}")
+                cols = slice(h * HALF, (h + 1) * HALF)
+                product(acc[:], w1_mx, t, x_codes[h][:], x_scale[:, cols])
+                copy = nc.scalar.copy if h == t else nc.vector.tensor_copy
+                copy(y[t][:, cols], acc[:])
+                if h == 0:
+                    scale_own(0, t, acc[:])
+                else:
+                    second_half.append(acc[:])
+        for t in range(2, PACK):
+            acc = bank(2 + t, [P, S], f"y_acc{t}")
             for h in range(2):
-                for t in (2 * pair, 2 * pair + 1):
-                    acc = bank(4 * h + t, [P, HALF], f"y_acc{h}{t}")
-                    cols = slice(h * HALF, (h + 1) * HALF)
-                    product(acc[:], w1_mx, t, x_codes[h][:], x_scale[:, cols])
-                    if h == 1 and t == 0:
-                        nc.vector.tensor_copy(y[t][:, cols], acc[:])
-                    else:
-                        nc.scalar.copy(y[t][:, cols], acc[:])
+                cols = slice(h * HALF, (h + 1) * HALF)
+                product(acc[:, cols], w1_mx, t, x_codes[h][:], x_scale[:, cols])
+            nc.scalar.copy(y[t][:], acc[:])
+            scale_own(0, t, acc[:, :HALF])
+            second_half.append(acc[:, HALF:])
         for t in range(PACK):
-            nc.scalar.activation(own[t][:], y[t][:], COPY, scale=eps_t[:, t : t + 1])
+            scale_own(1, t, second_half[t])
 
-        w3_grouped = tile([P, N, PACK], BF16, "w3_grouped")
-        for t in range(PACK):
-            cols = slice(P * t, P * (t + 1))
-            nc.gpsimd.tensor_scalar(
-                w3_grouped[:, cols, :], w3_raw[:, :, cols].rearrange("p j c -> p c j"), 1.0, 0.0, MULT, ADD
+        res_t = tile([P, PACK, S], F32, "res_t", "slot_c")
+        nc.sync.dma_start(res_t[:], res.rearrange("(p t) s -> p t s", t=PACK))
+        out_rows = out.rearrange("(p t) s -> p t s", t=PACK)
+
+        def neighbour_sums(h, tags):
+            z = tile([P, PACK, HALF], F32, f"z{h}")
+            places = slice(h * HALF // 16, (h + 1) * HALF // 16)
+            partial = []
+            for t in range(PACK + 1):
+                if t < PACK:
+                    partial.append(tile([P, HALF], F32, f"partial{h}{t}", tags[t]))
+                    nc.vector.tensor_tensor(partial[t][:], y[t][:].indirect(p1_t[:, places]), own[h][t][:], ADD)
+                if t > 0:
+                    nc.vector.tensor_tensor(
+                        z[:, t - 1, :], y[t - 1][:].indirect(p2_t[:, places]), partial[t - 1][:], ADD
+                    )
+            return z
+
+        def interleave(copy, z, lo, hi, name):
+            grouped = tile([P, (hi - lo) * PACK], BF16, name)
+            copy(
+                grouped[:].rearrange("p (c i t) -> p c t i", i=4, t=PACK),
+                z[:, :, lo:hi].rearrange("p t (c i) -> p c t i", i=4),
             )
+            return grouped[:]
 
-        def turn_into(acc, source, start, stop):
-            nc.tensor.matmul(acc, lhsT=source, rhs=ident[:], is_transpose=True, start=start, stop=stop)
-
-        def turn_back(b, z_turned):
-            z_rows = tile([P, 2, P, 2], BF16, f"z_rows{b}")
-            nc.scalar.copy(z_rows[:], z_turned[:].rearrange("s (u e) p -> s u p e", e=2))
-            words = z_rows[:].rearrange("s u p e -> s (u p e)").bitcast(F32)
-            back = bank(BACK_BANK[b], [P, 2, BLOCK], f"back{b}")
-            for u in range(2):
-                nc.tensor.transpose(back[:, u, :], words[:, u * P : (u + 1) * P], ident[:])
-            z_grouped = tile([P, BLOCK * PACK], BF16, f"z_grouped{b}")
-            nc.scalar.copy(
-                z_grouped[:].bitcast(F32).rearrange("p (s u) -> p s u", u=2),
-                back[:].rearrange("p u s -> p s u"),
-            )
-            return z_grouped
-
-        z_grouped = []
-        for lo, hi in PIECES:
-            z_turned = {}
-            for b in range(lo // BLOCK, hi // BLOCK):
-                z_turned[b] = bank(SUM_BANK[b], [P, PACK, P], f"z_turned{b}")
-                for t in range(PACK):
-                    turn_into(z_turned[b][:, t, :], own[t][:, b * BLOCK : (b + 1) * BLOCK], t == 0, False)
+        def hidden(b, codes, scales, grouped):
+            h_acc = bank(b, [P, PACK, BLOCK], f"h_acc{b}")
             for t in range(PACK):
-                for name, places in (("a", p1_t), ("b", p2_t)):
-                    fetched = tile([P, hi - lo], F32, f"fetched_{name}{t}_{lo}")
-                    nc.vector.tensor_copy(fetched[:], y[t][:].indirect(places[:, lo // 16 : hi // 16]))
-                    for c in range(lo, hi, BLOCK):
-                        turn_into(
-                            z_turned[c // BLOCK][:, t, :],
-                            fetched[:, c - lo : c - lo + BLOCK],
-                            False,
-                            t == PACK - 1 and name == "b",
-                        )
-            for b in range(lo // BLOCK, hi // BLOCK):
-                z_grouped.append(turn_back(b, z_turned[b]))
-
-        w2_halves = [deal_columns(nc.scalar.copy, w2_raw, u, f"w2_grouped{u}") for u in range(2)]
-        w2_mx = quantize_halves(w2_halves, "w2", "fetched_b3_384")
-        w3_mx = (tile([P, N], U32, "w3_codes", "z_rows3"), tile([P, N], U8, "w3_scales"))
-        quantize(w3_mx[0][:], w3_mx[1][:], w3_grouped[:].rearrange("p c j -> p (c j)"))
-
-        out_rows = out.rearrange("(t p) s -> p t s", t=PACK)
-        for b in range(BLOCKS):
-            cols = slice(b * BLOCK, (b + 1) * BLOCK)
-            z_codes = tile([P, BLOCK], U32, f"z_codes{b}")
-            z_scales = tile([P, BLOCK], U8, f"z_scales{b}")
-            quantize(z_codes[:], z_scales[:], z_grouped[b][:])
-            h_acc = bank(HIDDEN_BANK[b], [P, PACK, BLOCK], f"h_acc{b}")
-            for t in range(PACK):
-                product(h_acc[:, t, :], w2_mx, t, z_codes[:], z_scales[:])
-            h_grouped = tile([P, BLOCK * PACK], BF16, f"h_grouped{b}")
+                product(h_acc[:, t, :], w2_mx, t, codes, scales)
             nc.scalar.activation(
-                h_grouped[:].rearrange("p (s t) -> p s t", t=PACK),
-                h_acc[:].rearrange("p t s -> p s t"),
-                RELU,
+                grouped.rearrange("p (s t) -> p s t", t=PACK), h_acc[:].rearrange("p t s -> p s t"), RELU
             )
-            h_codes = tile([P, BLOCK], U32, f"h_codes{b}")
-            h_scales = tile([P, BLOCK], U8, f"h_scales{b}")
-            quantize(h_codes[:], h_scales[:], h_grouped[:])
-            o_acc = bank(OUT_BANK[b], [P, PACK, BLOCK], f"o_acc{b}")
+
+        def finish(acc, rows, cols, name):
+            result = tile(list(acc.shape), F32, name)
+            nc.vector.tensor_tensor(result[:], acc[:], res_t[:, rows, cols], ADD)
+            nc.sync.dma_start(out_rows[:, rows, cols], result[:])
+
+        z_first = neighbour_sums(0, [None] * PACK)
+        w2_mx = column_tiles(*quantized(deal_all_columns(w2_raw, "w2_grouped"), "w2"))
+        z_first_mx = column_tiles(
+            *quantized(interleave(nc.scalar.copy, z_first, 0, HALF, "z_first_grouped"), "z_first")
+        )
+        z_second = neighbour_sums(1, ["partial03", "partial02", "w2_grouped", "z_first_grouped"])
+        w3_grouped = deal_all_columns(w3_raw, "w3_grouped")
+        h_first = tile([P, HALF * PACK], BF16, "h_first")
+        for b in range(2):
+            hidden(b, *z_first_mx[b], h_first[:, b * BLOCK * PACK : (b + 1) * BLOCK * PACK])
+
+        z_late = {}
+        for b, copy in ((3, nc.vector.tensor_copy), (2, nc.scalar.copy)):
+            lo = (b - 2) * BLOCK
+            z_late[b] = quantized(interleave(copy, z_second, lo, lo + BLOCK, f"z_grouped{b}"), f"z{b}")
+        w3_mx = column_tiles(*quantized(w3_grouped, "w3"))
+
+        h_codes, h_scales = quantized(h_first[:], "h_first")
+        h_late = {}
+        for b in (3, 2):
+            h_late[b] = tile([P, BLOCK * PACK], BF16, f"h_grouped{b}")
+            hidden(b, z_late[b][0][:], z_late[b][1][:], h_late[b][:])
+        for pair in range(2):
+            o_acc = bank(6 + pair, [P, 2, HALF], f"o_first{pair}")
+            for e in range(2):
+                product(o_acc[:, e, :], w3_mx, 2 * pair + e, h_codes[:], h_scales[:])
+            finish(o_acc, slice(2 * pair, 2 * pair + 2), slice(0, HALF), f"result_first{pair}")
+        for b in (3, 2):
+            codes, scales = quantized(h_late[b][:], f"h{b}")
+            o_acc = bank(2 + b, [P, PACK, BLOCK], f"o_acc{b}")
             for t in range(PACK):
-                product(o_acc[:, t, :], w3_mx, t, h_codes[:], h_scales[:])
-            result = tile([P, PACK, BLOCK], F32, f"result{b}")
-            nc.vector.tensor_tensor(result[:], o_acc[:], res_t[:, :, cols], ADD)
-            nc.sync.dma_start(out_rows[:, :, cols], result[:])
+                product(o_acc[:, t, :], w3_mx, t, codes[:], scales[:])
+            finish(o_acc, slice(0, PACK), slice(b * BLOCK, (b + 1) * BLOCK), f"result{b}")

from contextlib import ExitStack

import concourse.mybir as mybir

K, T, S, H, N = 512, 2048, 512, 512, 512
FLOPS = 2 * S * (K * H + H * H + H * N)

F32 = mybir.dt.float32
BF16 = mybir.dt.bfloat16
I32 = mybir.dt.int32
U32 = mybir.dt.uint32
U16 = mybir.dt.uint16
U8 = mybir.dt.uint8
FP8X4 = mybir.dt.float8_e4m3fn_x4
COPY = mybir.ActivationFunctionType.Copy
RELU = mybir.ActivationFunctionType.Relu
ADD = mybir.AluOpType.add

P = 128
PACK = 4
HALF = S // 2
BLOCK = 128
BLOCKS = S // BLOCK


def tile_picked_gin8_relu_p_kernel(
    tc, x_words, x_scales, w1, eps, w2, res, w3, offs, p1, p2, out
):
    nc = tc.nc
    with ExitStack() as ctx:
        lists = ctx.enter_context(tc.tile_pool(name="lists", bufs=1))
        keep = ctx.enter_context(tc.tile_pool(name="keep", bufs=1))
        psum = ctx.enter_context(tc.psum_pool(name="psum", bufs=1))

        def bank(b, shape, name):
            return psum.tile(shape, F32, name=name, tag=f"bank{b}")

        def tile(shape, dtype, name, tag=None):
            return keep.tile(shape, dtype, name=name, tag=tag or name, align_bytes=64)

        offs_t = lists.tile([P, S // 16], U16, name="offs_t")
        p1_t = lists.tile([P, S // 16], U16, name="p1_t")
        p2_t = lists.tile([P, S // 16], U16, name="p2_t")

        x_table = tile([P, T], U32, "x_table", "slot_c")
        scale_table = tile([P, T], U8, "scale_table", "slot_a")
        w1_raw = tile([P, PACK, H], F32, "w1_raw", "slot_b")
        eps_t = tile([P, PACK], F32, "eps_t")

        nc.gpsimd.memset(scale_table[:].bitcast(I32), 0)

        nc.sync.dma_start(offs_t[:], offs)
        nc.sync.dma_start(w1_raw[:], w1.rearrange("(p j) c -> p j c", j=PACK))
        for q in range(4):
            nc.sync.dma_start(
                scale_table[32 * q : 32 * q + 4, :].bitcast(I32),
                x_scales[0, 4 * q : 4 * q + 4, :].bitcast(I32),
            )
        nc.sync.dma_start(
            x_table[:].bitcast(I32), x_words[0].rearrange("p n t -> p (n t)").bitcast(I32)
        )
        nc.sync.dma_start(p1_t[:], p1)
        nc.sync.dma_start(p2_t[:], p2)
        nc.gpsimd.dma_start(eps_t[:], eps.rearrange("(p t) o -> p (t o)", t=PACK))

        def product(acc, weights, t, codes, scales):
            lhs_codes, lhs_scales = weights[t]
            nc.tensor.matmul_mx(
                out=acc,
                lhsT=lhs_codes.bitcast(FP8X4),
                lhsT_scale=lhs_scales,
                rhs=codes.bitcast(FP8X4),
                rhs_scale=scales,
                start=True,
                stop=True,
            )

        def quantized(values, name, tag=None):
            width = values.shape[1] // PACK
            codes = tile([P, width], U32, name + "_codes", tag)
            scales = tile([P, width], U8, name + "_scales")
            nc.vector.quantize_mx(out=codes[:].bitcast(FP8X4), scales=scales[:], in_=values)
            return codes, scales

        def column_tiles(codes, scales):
            return [(codes[:, c : c + P], scales[:, c : c + P]) for c in range(0, codes.shape[1], P)]

        def deal_columns(raw, grouped, u):
            nc.scalar.activation(
                grouped.rearrange("p e m j -> p m j e"),
                raw[:].rearrange("p j (m t) -> p m j t", t=PACK)[:, :, :, 2 * u : 2 * u + 2],
                COPY,
            )

        def deal_all_columns(raw, name):
            grouped = tile([P, PACK, P, PACK], BF16, name)
            nc.scalar.activation(
                grouped[:].rearrange("p t m j -> p m j t"),
                raw[:].rearrange("p j (m t) -> p m j t", t=PACK),
                COPY,
            )
            return grouped[:].rearrange("p t m j -> p (t m j)")

        x_scale = tile([P, S], U8, "x_scale")
        nc.vector.tensor_copy(x_scale[:], scale_table[:].indirect(offs_t[:]))
        w1_grouped = [tile([P, 2, P, PACK], BF16, f"w1_grouped{u}") for u in range(2)]
        for u in range(2):
            deal_columns(w1_raw, w1_grouped[u][:], u)
        w1_mx = column_tiles(*quantized(w1_grouped[0][:].rearrange("p e m j -> p (e m j)"), "w1_low"))

        x_codes = []
        for h in range(2):
            codes = tile([P, HALF], U32, f"x_codes{h}", ("x_codes0", "w2_grouped")[h])
            nc.vector.tensor_copy(
                codes[:], x_table[:].indirect(offs_t[:, h * HALF // 16 : (h + 1) * HALF // 16])
            )
            x_codes.append(codes)

        w1_mx = w1_mx + column_tiles(
            *quantized(w1_grouped[1][:].rearrange("p e m j -> p (e m j)"), "w1_high", "slot_c")
        )

        w2_raw = tile([P, PACK, H], F32, "w2_raw", "slot_a")
        nc.sync.dma_start(w2_raw[:], w2.rearrange("(p j) c -> p j c", j=PACK))
        w3_raw = tile([P, PACK, N], F32, "w3_raw", "slot_b")
        nc.sync.dma_start(w3_raw[:], w3.rearrange("(p j) c -> p j c", j=PACK))

        y = [tile([P, S], F32, f"y{t}") for t in range(PACK)]
        own = [[tile([P, HALF], F32, f"own{h}{t}") for t in range(PACK)] for h in range(2)]

        def scale_own(h, t, acc):
            nc.scalar.activation(own[h][t][:], acc, COPY, scale=eps_t[:, t : t + 1])

        second_half = []
        for h in range(2):
            for t in range(2):
                acc = bank(2 * h + t, [P, HALF], f"y_acc{h}{t}")
                cols = slice(h * HALF, (h + 1) * HALF)
                product(acc[:], w1_mx, t, x_codes[h][:], x_scale[:, cols])
                copy = nc.scalar.copy if h == t else nc.vector.tensor_copy
                copy(y[t][:, cols], acc[:])
                if h == 0:
                    scale_own(0, t, acc[:])
                else:
                    second_half.append(acc[:])
        for t in range(2, PACK):
            acc = bank(2 + t, [P, S], f"y_acc{t}")
            for h in range(2):
                cols = slice(h * HALF, (h + 1) * HALF)
                product(acc[:, cols], w1_mx, t, x_codes[h][:], x_scale[:, cols])
            nc.scalar.copy(y[t][:], acc[:])
            scale_own(0, t, acc[:, :HALF])
            second_half.append(acc[:, HALF:])
        for t in range(PACK):
            scale_own(1, t, second_half[t])

        res_t = tile([P, PACK, S], F32, "res_t", "slot_c")
        nc.sync.dma_start(res_t[:], res.rearrange("(p t) s -> p t s", t=PACK))
        out_rows = out.rearrange("(p t) s -> p t s", t=PACK)

        def neighbour_sums(h, tags):
            z = tile([P, PACK, HALF], F32, f"z{h}")
            places = slice(h * HALF // 16, (h + 1) * HALF // 16)
            partial = []
            for t in range(PACK + 1):
                if t < PACK:
                    partial.append(tile([P, HALF], F32, f"partial{h}{t}", tags[t]))
                    nc.vector.tensor_tensor(partial[t][:], y[t][:].indirect(p1_t[:, places]), own[h][t][:], ADD)
                if t > 0:
                    nc.vector.tensor_tensor(
                        z[:, t - 1, :], y[t - 1][:].indirect(p2_t[:, places]), partial[t - 1][:], ADD
                    )
            return z

        def interleave(copy, z, lo, hi, name):
            grouped = tile([P, (hi - lo) * PACK], BF16, name)
            copy(
                grouped[:].rearrange("p (c i t) -> p c t i", i=4, t=PACK),
                z[:, :, lo:hi].rearrange("p t (c i) -> p c t i", i=4),
            )
            return grouped[:]

        def hidden(b, codes, scales, grouped):
            h_acc = bank(b, [P, PACK, BLOCK], f"h_acc{b}")
            for t in range(PACK):
                product(h_acc[:, t, :], w2_mx, t, codes, scales)
            nc.scalar.activation(
                grouped.rearrange("p (s t) -> p s t", t=PACK), h_acc[:].rearrange("p t s -> p s t"), RELU
            )

        def finish(acc, rows, cols, name):
            result = tile(list(acc.shape), F32, name)
            nc.vector.tensor_tensor(result[:], acc[:], res_t[:, rows, cols], ADD)
            nc.sync.dma_start(out_rows[:, rows, cols], result[:])

        z_first = neighbour_sums(0, [None] * PACK)
        w2_mx = column_tiles(*quantized(deal_all_columns(w2_raw, "w2_grouped"), "w2"))
        z_first_mx = column_tiles(
            *quantized(interleave(nc.scalar.copy, z_first, 0, HALF, "z_first_grouped"), "z_first")
        )
        z_second = neighbour_sums(1, ["partial03", "partial02", "w2_grouped", "z_first_grouped"])
        w3_grouped = deal_all_columns(w3_raw, "w3_grouped")
        h_first = tile([P, HALF * PACK], BF16, "h_first")
        for b in range(2):
            hidden(b, *z_first_mx[b], h_first[:, b * BLOCK * PACK : (b + 1) * BLOCK * PACK])

        z_late = {}
        for b, copy in ((3, nc.vector.tensor_copy), (2, nc.scalar.copy)):
            lo = (b - 2) * BLOCK
            z_late[b] = quantized(interleave(copy, z_second, lo, lo + BLOCK, f"z_grouped{b}"), f"z{b}")
        w3_mx = column_tiles(*quantized(w3_grouped, "w3"))

        h_codes, h_scales = quantized(h_first[:], "h_first")
        h_late = {}
        for b in (3, 2):
            h_late[b] = tile([P, BLOCK * PACK], BF16, f"h_grouped{b}")
            hidden(b, z_late[b][0][:], z_late[b][1][:], h_late[b][:])
        for pair in range(2):
            o_acc = bank(6 + pair, [P, 2, HALF], f"o_first{pair}")
            for e in range(2):
                product(o_acc[:, e, :], w3_mx, 2 * pair + e, h_codes[:], h_scales[:])
            finish(o_acc, slice(2 * pair, 2 * pair + 2), slice(0, HALF), f"result_first{pair}")
        for b in (3, 2):
            codes, scales = quantized(h_late[b][:], f"h{b}")
            o_acc = bank(2 + b, [P, PACK, BLOCK], f"o_acc{b}")
            for t in range(PACK):
                product(o_acc[:, t, :], w3_mx, t, codes[:], scales[:])
            finish(o_acc, slice(0, PACK), slice(b * BLOCK, (b + 1) * BLOCK), f"result{b}")
